import numpy as np
import ml_dtypes


def mxq(x, axis, fmt="e4m3"):
    dtype, down = {"e4m3": (ml_dtypes.float8_e4m3fn, 7), "e5m2": (ml_dtypes.float8_e5m2, 14)}[fmt]
    v = np.moveaxis(np.asarray(x, np.float32).astype(ml_dtypes.bfloat16).astype(np.float64), axis, -1)
    blocks = v.reshape(v.shape[:-1] + (-1, 32))
    amax = np.abs(blocks).max(-1, keepdims=True)
    byte = np.maximum(np.where(amax > 0, np.frexp(amax)[1] - 1 + 127, 0) - down, 1)
    scale = np.exp2(byte - 127.0)
    codes = (blocks / scale).astype(np.float32).astype(dtype).astype(np.float64)
    return np.moveaxis((codes * scale).reshape(v.shape), -1, axis)


WIDE = False


def mx_kscale(k):
    if not WIDE:
        return np.ones(k)
    levels = np.array([10, -10, 5, -5, 0])
    if k % 512:
        return np.exp2(np.random.permutation(np.resize(levels, k // 32))).repeat(32)
    a = np.empty((k // 512, 16))
    for p in range(k // 512):
        a[p, :8] = np.random.permutation(np.resize(levels, 8))
        for g in range(8):
            far = levels[np.abs(levels - a[p, g]) >= 10]
            a[p, g + 8] = far[np.random.randint(len(far))]
    return np.exp2(a.ravel()).repeat(32)


def f64(x):
    return np.asarray(x).astype(np.float64)


def striped(idx):
    return np.tile(idx.reshape(-1, 16).T, (8, 1)).astype(np.uint16)


def unstriped(offs):
    return offs[:16].T.reshape(-1).astype(np.int64)


E2M1 = np.array([0.0, 0.5, 1.0, 1.5, 2.0, 3.0, 4.0, 6.0, -0.0, -0.5, -1.0, -1.5, -2.0, -3.0, -4.0, -6.0])


def pack_weight(w, fmt):
    k, n = w.shape
    w = f64(np.asarray(w, np.float32).astype(ml_dtypes.bfloat16)).reshape(k // 32, 32, n)
    amax = np.abs(w).max(1)
    if fmt == "e4m3":
        byte = np.frexp(amax)[1] - 1 + 127 - 7
    else:
        mant, ex = np.frexp(amax / 6.0)
        byte = np.where(mant > 0.5, ex, ex - 1) + 127
    byte = np.clip(np.where(amax > 0, byte, 1), 1, 254)
    scaled = (w * np.exp2(127.0 - byte)[:, None, :]).reshape(k, n).astype(np.float32)
    by_word = np.ascontiguousarray(scaled.reshape(k // 512, 128, 4, n).transpose(0, 1, 3, 2))
    if fmt == "e4m3":
        words = by_word.astype(ml_dtypes.float8_e4m3fn).view(np.uint8)
    else:
        c = by_word.astype(ml_dtypes.float4_e2m1fn).view(np.uint8) & 0xF
        words = (c[..., 0::2] | (c[..., 1::2] << 4)).reshape(k // 512, 128, 2 * n)
    return np.ascontiguousarray(words), np.ascontiguousarray(byte.astype(np.uint8).reshape(k // 512, 16, n))


def unpack_weight(words, scales, fmt):
    g, _, n = scales.shape
    words = np.ascontiguousarray(words).reshape(g, 128, n, -1)
    if fmt == "e4m3":
        vals = words.view(ml_dtypes.float8_e4m3fn).astype(np.float64)
    else:
        nib = np.empty((g, 128, n, 4), np.uint8)
        nib[..., 0::2] = words & 0xF
        nib[..., 1::2] = words >> 4
        vals = E2M1[nib]
    vals = vals * np.repeat(np.exp2(scales.astype(np.float64) - 127.0), 8, axis=1)[..., None]
    return vals.transpose(0, 1, 3, 2).reshape(g * 512, n)


def gelu(v):
    return 0.5 * v * (1.0 + np.tanh(np.sqrt(2.0 / np.pi) * (v + 0.044715 * v**3)))


K, T, S, P, H, N = 1024, 2048, 1024, 512, 1024, 384

def setup_inputs():
    n = np.random.standard_normal
    s = mx_kscale(K)[:, None]
    u = mx_kscale(H)[:, None]
    tab_words, tab_scales = pack_weight(n((K, T)) * s, "e4m3")
    w2_words, w2_scales = pack_weight(0.8 * n((K, H)) / np.sqrt(K) / s, "e2m1")
    w4_words, w4_scales = pack_weight(n((H, N)) / np.sqrt(H) / u, "e4m3")
    return {
        "tab_words": tab_words, "tab_scales": tab_scales,
        "offs": striped(np.random.permutation(T)[:S]),
        "pos1": striped(np.random.permutation(S)[:P]),
        "pos2": striped(np.random.permutation(S)[:P]),
        "w1": (0.8 * n((K, H)) / np.sqrt(K) / s).astype(np.float32),
        "b1": (0.5 * n(H)).astype(np.float32),
        "w2_words": w2_words, "w2_scales": w2_scales,
        "slope": np.random.uniform(0.6, 3.0, H).astype(np.float32),
        "shift": n(H).astype(np.float32),
        "light": (2.0 * np.exp(0.4 * n((H, P))) * u).astype(np.float32),
        "w3": (n((H, N)) / np.sqrt(H) / u).astype(np.float32),
        "w4_words": w4_words, "w4_scales": w4_scales,
    }

def reference(tab_words, tab_scales, offs, pos1, pos2, w1, b1, w2_words, w2_scales,
              slope, shift, light, w3, w4_words, w4_scales):
    v = unpack_weight(tab_words, tab_scales, "e4m3")[:, unstriped(offs)]
    w2 = unpack_weight(w2_words, w2_scales, "e2m1")
    w4 = unpack_weight(w4_words, w4_scales, "e4m3")
    first = (mxq(f64(w1), 0, "e4m3").T @ v) + f64(b1)[:, None]
    h = np.minimum(first, w2.T @ v)
    a = 1.0 / (1.0 + np.exp(-(f64(slope)[:, None] * h[:, unstriped(pos1)] + f64(shift)[:, None])))
    q = a * h[:, unstriped(pos2)] * f64(light)
    qq = mxq(q, 0, "e4m3")
    y1 = mxq(f64(w3), 0, "e4m3").T @ qq
    y2 = w4.T @ qq
    return y1 + np.abs(y2)

@@ -1,0 +1,328 @@
+from contextlib import ExitStack
+
+import concourse.mybir as mybir
+
+K, T, S, PICK, H, N = 1024, 2048, 1024, 512, 1024, 384
+FLOPS = 2 * 2 * K * H * S + 2 * 2 * H * N * PICK
+
+F32 = mybir.dt.float32
+BF16 = mybir.dt.bfloat16
+I32 = mybir.dt.int32
+U32 = mybir.dt.uint32
+U16 = mybir.dt.uint16
+U8 = mybir.dt.uint8
+FP8X4 = mybir.dt.float8_e4m3fn_x4
+FP4X4 = mybir.dt.float4_e2m1fn_x4
+ALU = mybir.AluOpType
+ACT = mybir.ActivationFunctionType
+
+P = 128
+PACK = 4
+PASS = P * PACK
+BANK = 512
+QUADS = 4
+
+
+def tile_list_pack_mismatch_scores_kernel(
+    tc, tab_words, tab_scales, offs, pos1, pos2, w1, b1, w2_words, w2_scales,
+    slope, shift, light, w3, w4_words, w4_scales, out,
+):
+    nc = tc.nc
+    k_passes = K // PASS
+    r_passes = H // PASS
+    halves = S // BANK
+    n_tiles = N // P
+
+    with ExitStack() as ctx:
+        lists = ctx.enter_context(tc.tile_pool(name="lists", bufs=1))
+        keep = ctx.enter_context(tc.tile_pool(name="keep", bufs=1))
+        ring = ctx.enter_context(tc.tile_pool(name="ring", bufs=3))
+        psum = ctx.enter_context(tc.psum_pool(name="psum", bufs=8))
+
+        def kept(name, shape, dtype):
+            return keep.tile(shape, dtype, name=name, align_bytes=64)
+
+        def load_scale_rows(queue, plane, scales):
+            for q in range(QUADS):
+                queue.dma_start(
+                    out=plane[32 * q : 32 * q + 4, :, :].bitcast(I32),
+                    in_=scales[:, 4 * q : 4 * q + 4, :].rearrange("a r c -> r a c").bitcast(I32),
+                )
+
+        offs_sb = lists.tile([P, S // 16], U16, name="offs_sb")
+        pos1_sb = lists.tile([P, PICK // 16], U16, name="pos1_sb")
+        pos2_sb = lists.tile([P, PICK // 16], U16, name="pos2_sb")
+
+        tab_plane = kept("tab_plane", [P, k_passes, T], U8)
+        w2_plane_raw = kept("w2_plane_raw", [P, k_passes, H], U8)
+        w4_plane = kept("w4_plane", [P, r_passes, N], U8)
+        for plane in (tab_plane, w2_plane_raw, w4_plane):
+            nc.gpsimd.memset(plane[:].bitcast(I32), 0)
+
+        tab_sb = [kept("tab%d" % a, [P, T], U32) for a in range(k_passes)]
+        w1_raw = {(a, b): kept("w1raw%d%d" % (a, b), [P, PACK, PASS], F32) for a in range(k_passes) for b in range(r_passes)}
+        w2_raw = kept("w2_raw", [P, k_passes, 2 * H], U8)
+        light_sb = [kept("light%d" % b, [P, PACK, PICK], F32) for b in range(r_passes)]
+        w3_raw = [kept("w3raw%d" % b, [P, PACK, N], F32) for b in range(r_passes)]
+        w4_sb = kept("w4_sb", [P, r_passes, N], U32)
+        b1_sb = kept("b1_sb", [P, r_passes, PACK], F32)
+        slope_sb = kept("slope_sb", [P, r_passes, PACK], F32)
+        shift_sb = kept("shift_sb", [P, r_passes, PACK], F32)
+
+        def load_tab(a):
+            nc.sync.dma_start(out=tab_sb[a][:].bitcast(I32), in_=tab_words[a].rearrange("p t i -> p (t i)").bitcast(I32))
+
+        def load_w1(a, b):
+            rows = w1[a * PASS : (a + 1) * PASS, b * PASS : (b + 1) * PASS]
+            nc.sync.dma_start(out=w1_raw[a, b][:], in_=rows.rearrange("(p j) c -> p j c", j=PACK))
+
+        def load_rows(tile, matrix, b):
+            nc.sync.dma_start(out=tile[:], in_=matrix[b * PASS : (b + 1) * PASS, :].rearrange("(p j) c -> p j c", j=PACK))
+
+        def load_vector(tile, vec):
+            nc.sync.dma_start(out=tile[:], in_=vec.rearrange("(b p i) -> p b i", b=r_passes, i=PACK))
+
+        nc.sync.dma_start(offs_sb[:], offs)
+        nc.sync.dma_start(out=w2_raw[:].bitcast(I32), in_=w2_words.rearrange("a p c -> p a c").bitcast(I32))
+        load_vector(b1_sb, b1)
+        load_scale_rows(nc.sync, tab_plane, tab_scales)
+        load_tab(0)
+        load_w1(0, 0)
+        load_scale_rows(nc.sync, w2_plane_raw, w2_scales)
+        load_w1(1, 0)
+        load_tab(1)
+        nc.sync.dma_start(pos2_sb[:], pos2)
+        load_rows(light_sb[0], light, 0)
+        nc.sync.dma_start(pos1_sb[:], pos1)
+        load_vector(slope_sb, slope)
+        load_vector(shift_sb, shift)
+        load_w1(0, 1)
+        load_w1(1, 1)
+        load_rows(light_sb[1], light, 1)
+        load_rows(w3_raw[0], w3, 0)
+        load_rows(w3_raw[1], w3, 1)
+        nc.sync.dma_start(out=w4_sb[:].bitcast(I32), in_=w4_words.rearrange("a p c i -> p a (c i)").bitcast(I32))
+        load_scale_rows(nc.sync, w4_plane, w4_scales)
+
+        w2_sb = kept("w2_sb", [P, k_passes, 2 * H], U8)
+        w2_plane = kept("w2_plane", [P, k_passes, H], U8)
+        nc.scalar.copy(
+            out=w2_sb[:].bitcast(U16).rearrange("p a (b t m) -> p (a b) t m", b=r_passes, t=PACK),
+            in_=w2_raw[:].bitcast(U16).rearrange("p a (b m t) -> p (a b) t m", b=r_passes, t=PACK),
+        )
+        for b in range(r_passes):
+            cols = slice(b * PASS, (b + 1) * PASS)
+            nc.gpsimd.tensor_copy(
+                out=w2_plane[:, :, cols].rearrange("p a (t m) -> p a t m", t=PACK),
+                in_=w2_plane_raw[:, :, cols].rearrange("p a (m t) -> p a t m", t=PACK),
+            )
+
+        v_codes = [kept("vcodes%d" % a, [P, S], U32) for a in range(k_passes)]
+        v_plane = [kept("vplane%d" % a, [P, S], U8) for a in range(k_passes)]
+
+        def gather_plane(a):
+            nc.vector.tensor_copy(out=v_plane[a][:], in_=tab_plane[:, a, :].indirect(offs_sb[:]))
+
+        def gather_codes(a, half):
+            nc.vector.tensor_copy(
+                out=v_codes[a][:, half * BANK : (half + 1) * BANK],
+                in_=tab_sb[a][:].indirect(offs_sb[:, half * BANK // 16 : (half + 1) * BANK // 16]),
+            )
+
+        w1_bf = {}
+        w1_codes = {}
+        w1_plane = {}
+
+        for a in range(k_passes):
+            for b in range(r_passes):
+                w1_bf[a, b] = kept("w1bf%d%d" % (a, b), [P, PASS * PACK], BF16)
+
+        def round_w1(a, b, u):
+            nc.scalar.copy(
+                out=w1_bf[a, b][:].rearrange("p (u e m j) -> p u m j e", u=2, e=2, j=PACK)[:, u],
+                in_=w1_raw[a, b][:].rearrange("p j (m u e) -> p u m j e", u=2, e=2)[:, u],
+            )
+
+        def quantise(name, tile, width):
+            codes = kept(name + "c", [P, width], U32)
+            plane = kept(name + "s", [P, width], U8)
+            nc.vector.quantize_mx(out=codes[:].bitcast(FP8X4), scales=plane[:], in_=tile[:])
+            return codes, plane
+
+        def quantise_w1(a, b):
+            w1_codes[a, b], w1_plane[a, b] = quantise("w1q%d%d" % (a, b), w1_bf[a, b], PASS)
+
+        def woven(tile):
+            return tile[:].rearrange("p (c e t) -> p c t e", e=2, t=PACK)
+
+        def by_pairs(tile):
+            return tile[:].rearrange("p t (c e) -> p c t e", e=2)
+
+        w3_bf = {}
+        w3_q = {}
+
+        def round_w3(b):
+            tile = kept("w3bf%d" % b, [P, N * PACK], BF16)
+            nc.scalar.copy(out=woven(tile), in_=by_pairs(w3_raw[b]))
+            w3_bf[b] = tile
+
+        def quantise_w3(b):
+            w3_q[b] = quantise("w3q%d" % b, w3_bf[b], N)
+
+        h_tiles = {}
+
+        def first_stage(b, i):
+            h = ring.tile([P, S], F32, name="h", bufs=8)
+            cols = slice(i * P, (i + 1) * P)
+            col2 = b * PASS + i * P
+            for half in range(halves):
+                js = slice(half * BANK, (half + 1) * BANK)
+                second = psum.tile([P, BANK], F32, name="acc")
+                first = psum.tile([P, BANK], F32, name="acc")
+                for a in range(k_passes):
+                    nc.tensor.matmul_mx(
+                        out=second[:],
+                        lhsT=w2_sb[:, a, 2 * col2 : 2 * (col2 + P)].bitcast(FP4X4),
+                        lhsT_scale=w2_plane[:, a, col2 : col2 + P],
+                        rhs=v_codes[a][:, js].bitcast(FP8X4),
+                        rhs_scale=v_plane[a][:, js],
+                        start=(a == 0), stop=(a == k_passes - 1),
+                    )
+                for a in range(k_passes):
+                    nc.tensor.matmul_mx(
+                        out=first[:],
+                        lhsT=w1_codes[a, b][:, cols].bitcast(FP8X4),
+                        lhsT_scale=w1_plane[a, b][:, cols],
+                        rhs=v_codes[a][:, js].bitcast(FP8X4),
+                        rhs_scale=v_plane[a][:, js],
+                        start=(a == 0), stop=(a == k_passes - 1),
+                    )
+                nc.scalar.copy(out=h[:, js], in_=second[:])
+                nc.vector.scalar_tensor_tensor(
+                    out=h[:, js], in0=first[:], scalar=b1_sb[:, b, i : i + 1], in1=h[:, js], op0=ALU.add, op1=ALU.min
+                )
+            h_tiles[b, i] = h
+
+        gate = [kept("gate%d" % b, [P, PACK, PICK], F32) for b in range(r_passes)]
+        lit = [kept("lit%d" % b, [P, PACK, PICK], F32) for b in range(r_passes)]
+
+        def look(b, i, lo=0, hi=PICK):
+            nc.scalar.activation(
+                out=gate[b][:, i, lo:hi], in_=h_tiles[b, i][:].indirect(pos1_sb[:, lo // 16 : hi // 16]), func=ACT.Sigmoid,
+                bias=shift_sb[:, b, i : i + 1], scale=slope_sb[:, b, i : i + 1],
+            )
+
+        def pick(b, i, lo=0, hi=PICK):
+            nc.vector.tensor_tensor(
+                out=lit[b][:, i, lo:hi], in0=h_tiles[b, i][:].indirect(pos2_sb[:, lo // 16 : hi // 16]),
+                in1=light_sb[b][:, i, lo:hi], op=ALU.mult,
+            )
+
+        HALF = PICK // 2
+        q_bf = [kept("qbf%d" % b, [P, PICK * PACK], BF16) for b in range(r_passes)]
+        q_codes = [kept("qc%d" % b, [P, PICK], U32) for b in range(r_passes)]
+        q_plane = [kept("qs%d" % b, [P, PICK], U8) for b in range(r_passes)]
+
+        def round_q(b, half):
+            pairs = slice(half * HALF // 2, (half + 1) * HALF // 2)
+            nc.vector.tensor_tensor(
+                out=woven(q_bf[b])[:, pairs], in0=by_pairs(lit[b])[:, pairs], in1=by_pairs(gate[b])[:, pairs], op=ALU.mult
+            )
+
+        def quantise_q(b, half):
+            ms = slice(half * HALF, (half + 1) * HALF)
+            nc.vector.quantize_mx(
+                out=q_codes[b][:, ms].bitcast(FP8X4), scales=q_plane[b][:, ms],
+                in_=q_bf[b][:, half * HALF * PACK : (half + 1) * HALF * PACK],
+            )
+
+        sums = {}
+
+        def second_stage(b, half):
+            ms = slice(half * HALF, (half + 1) * HALF)
+            w3_codes, w3_plane = w3_q[b]
+            for n in range(n_tiles):
+                cols = slice(n * P, (n + 1) * P)
+                if b == 0:
+                    sums[half, n] = psum.tile([P, 2, HALF], F32, name="acc")
+                bank = sums[half, n]
+                nc.tensor.matmul_mx(
+                    out=bank[:, 1, :], lhsT=w4_sb[:, b, cols].bitcast(FP8X4), lhsT_scale=w4_plane[:, b, cols],
+                    rhs=q_codes[b][:, ms].bitcast(FP8X4), rhs_scale=q_plane[b][:, ms], start=(b == 0), stop=False,
+                )
+                nc.tensor.matmul_mx(
+                    out=bank[:, 0, :], lhsT=w3_codes[:, cols].bitcast(FP8X4), lhsT_scale=w3_plane[:, cols],
+                    rhs=q_codes[b][:, ms].bitcast(FP8X4), rhs_scale=q_plane[b][:, ms], start=False, stop=(b == r_passes - 1),
+                )
+
+        def finish(half):
+            for n in range(n_tiles):
+                bank = sums[half, n]
+                res = ring.tile([P, HALF], F32, name="res", bufs=6)
+                nc.scalar.activation(out=res[:], in_=bank[:, 1, :], func=ACT.Abs)
+                nc.vector.tensor_tensor(out=res[:], in0=bank[:, 0, :], in1=res[:], op=ALU.add)
+                nc.sync.dma_start(out=out[n * P : (n + 1) * P, half * HALF : (half + 1) * HALF], in_=res[:])
+
+        gather_plane(0)
+        gather_codes(0, 0)
+        gather_codes(0, 1)
+        gather_plane(1)
+        round_w1(0, 0, 0)
+        round_w1(0, 0, 1)
+        quantise_w1(0, 0)
+        round_w1(1, 0, 0)
+        round_w1(1, 0, 1)
+        quantise_w1(1, 0)
+        gather_codes(1, 0)
+        gather_codes(1, 1)
+
+        first_stage(0, 0)
+        first_stage(0, 1)
+        pick(0, 0)
+        first_stage(0, 2)
+        round_w1(0, 1, 0)
+        round_w1(0, 1, 1)
+        quantise_w1(0, 1)
+        pick(0, 1)
+        first_stage(0, 3)
+        round_w1(1, 1, 0)
+        round_w1(1, 1, 1)
+        quantise_w1(1, 1)
+        pick(0, 2)
+        first_stage(1, 0)
+        pick(0, 3)
+        first_stage(1, 1)
+        pick(1, 0)
+        first_stage(1, 2)
+        pick(1, 1)
+        first_stage(1, 3)
+        look(0, 0)
+        look(0, 1)
+        look(0, 2)
+        look(0, 3)
+        pick(1, 2)
+        round_q(0, 0)
+        round_w3(0)
+        look(1, 0)
+        look(1, 1)
+        pick(1, 3, 0, HALF)
+        quantise_q(0, 0)
+        round_q(0, 1)
+        look(1, 2)
+        look(1, 3, 0, HALF)
+        round_w3(1)
+        look(1, 3, HALF, PICK)
+        quantise_w3(0)
+        quantise_q(0, 1)
+        second_stage(0, 0)
+        second_stage(0, 1)
+        round_q(1, 0)
+        pick(1, 3, HALF, PICK)
+        quantise_q(1, 0)
+        quantise_w3(1)
+        second_stage(1, 0)
+        round_q(1, 1)
+        quantise_q(1, 1)
+        second_stage(1, 1)
+        finish(0)
+        finish(1)

@@ -37,7 +37,7 @@ def tile_list_pack_mismatch_scores_kernel(
         lists = ctx.enter_context(tc.tile_pool(name="lists", bufs=1))
         keep = ctx.enter_context(tc.tile_pool(name="keep", bufs=1))
         ring = ctx.enter_context(tc.tile_pool(name="ring", bufs=3))
-        psum = ctx.enter_context(tc.psum_pool(name="psum", bufs=8))
+        psum = ctx.enter_context(tc.psum_pool(name="psum", bufs=4))
 
         def kept(name, shape, dtype):
             return keep.tile(shape, dtype, name=name, align_bytes=64)
@@ -53,10 +53,11 @@ def tile_list_pack_mismatch_scores_kernel(
         pos1_sb = lists.tile([P, PICK // 16], U16, name="pos1_sb")
         pos2_sb = lists.tile([P, PICK // 16], U16, name="pos2_sb")
 
-        tab_plane = kept("tab_plane", [P, k_passes, T], U8)
+        tab_plane = kept("tab_plane", [P, T], U8)
+        v_plane_moved = kept("v_plane_moved", [P, S], U8)
         w2_plane_raw = kept("w2_plane_raw", [P, k_passes, H], U8)
         w4_plane = kept("w4_plane", [P, r_passes, N], U8)
-        for plane in (tab_plane, w2_plane_raw, w4_plane):
+        for plane in (tab_plane, w2_plane_raw, v_plane_moved, w4_plane):
             nc.gpsimd.memset(plane[:].bitcast(I32), 0)
 
         tab_sb = [kept("tab%d" % a, [P, T], U32) for a in range(k_passes)]
@@ -85,12 +86,23 @@ def tile_list_pack_mismatch_scores_kernel(
         nc.sync.dma_start(offs_sb[:], offs)
         nc.sync.dma_start(out=w2_raw[:].bitcast(I32), in_=w2_words.rearrange("a p c -> p a c").bitcast(I32))
         load_vector(b1_sb, b1)
-        load_scale_rows(nc.sync, tab_plane, tab_scales)
+        for q in range(QUADS):
+            nc.sync.dma_start(
+                out=tab_plane[32 * q : 32 * q + 4 * k_passes, :].bitcast(I32),
+                in_=tab_scales[:, 4 * q : 4 * q + 4, :].bitcast(I32),
+            )
         load_tab(0)
         load_w1(0, 0)
         load_scale_rows(nc.sync, w2_plane_raw, w2_scales)
         load_w1(1, 0)
         load_tab(1)
+        v_plane = kept("v_plane", [P, S], U8)
+        nc.vector.tensor_copy(out=v_plane[:], in_=tab_plane[:].indirect(offs_sb[:]))
+        for q in range(QUADS):
+            nc.sync.dma_start(
+                out=v_plane_moved[32 * q : 32 * q + 4, :].bitcast(I32),
+                in_=v_plane[32 * q + 4 : 32 * q + 8, :].bitcast(I32),
+            )
         nc.sync.dma_start(pos2_sb[:], pos2)
         load_rows(light_sb[0], light, 0)
         nc.sync.dma_start(pos1_sb[:], pos1)
@@ -110,18 +122,14 @@ def tile_list_pack_mismatch_scores_kernel(
             out=w2_sb[:].bitcast(U16).rearrange("p a (b t m) -> p (a b) t m", b=r_passes, t=PACK),
             in_=w2_raw[:].bitcast(U16).rearrange("p a (b m t) -> p (a b) t m", b=r_passes, t=PACK),
         )
-        for b in range(r_passes):
-            cols = slice(b * PASS, (b + 1) * PASS)
-            nc.gpsimd.tensor_copy(
-                out=w2_plane[:, :, cols].rearrange("p a (t m) -> p a t m", t=PACK),
-                in_=w2_plane_raw[:, :, cols].rearrange("p a (m t) -> p a t m", t=PACK),
+
+        def deal_w2_plane():
+            nc.vector.tensor_copy(
+                out=w2_plane[:].rearrange("p a (b t m) -> p (a b) t m", b=r_passes, t=PACK),
+                in_=w2_plane_raw[:].rearrange("p a (b m t) -> p (a b) t m", b=r_passes, t=PACK),
             )
 
         v_codes = [kept("vcodes%d" % a, [P, S], U32) for a in range(k_passes)]
-        v_plane = [kept("vplane%d" % a, [P, S], U8) for a in range(k_passes)]
-
-        def gather_plane(a):
-            nc.vector.tensor_copy(out=v_plane[a][:], in_=tab_plane[:, a, :].indirect(offs_sb[:]))
 
         def gather_codes(a, half):
             nc.vector.tensor_copy(
@@ -137,8 +145,8 @@ def tile_list_pack_mismatch_scores_kernel(
             for b in range(r_passes):
                 w1_bf[a, b] = kept("w1bf%d%d" % (a, b), [P, PASS * PACK], BF16)
 
-        def round_w1(a, b, u):
-            nc.scalar.copy(
+        def round_w1(a, b, u, copy=nc.scalar.copy):
+            copy(
                 out=w1_bf[a, b][:].rearrange("p (u e m j) -> p u m j e", u=2, e=2, j=PACK)[:, u],
                 in_=w1_raw[a, b][:].rearrange("p j (m u e) -> p u m j e", u=2, e=2)[:, u],
             )
@@ -171,37 +179,46 @@ def tile_list_pack_mismatch_scores_kernel(
 
         h_tiles = {}
 
-        def first_stage(b, i):
+        def reading_w2(b, i):
             h = ring.tile([P, S], F32, name="h", bufs=8)
-            cols = slice(i * P, (i + 1) * P)
             col2 = b * PASS + i * P
             for half in range(halves):
                 js = slice(half * BANK, (half + 1) * BANK)
-                second = psum.tile([P, BANK], F32, name="acc")
-                first = psum.tile([P, BANK], F32, name="acc")
+                second = psum.tile([P, BANK], F32, name="bank_a")
                 for a in range(k_passes):
                     nc.tensor.matmul_mx(
                         out=second[:],
                         lhsT=w2_sb[:, a, 2 * col2 : 2 * (col2 + P)].bitcast(FP4X4),
                         lhsT_scale=w2_plane[:, a, col2 : col2 + P],
                         rhs=v_codes[a][:, js].bitcast(FP8X4),
-                        rhs_scale=v_plane[a][:, js],
+                        rhs_scale=(v_plane, v_plane_moved)[a][:, js],
                         start=(a == 0), stop=(a == k_passes - 1),
                     )
+                nc.scalar.copy(out=h[:, js], in_=second[:])
+            h_tiles[b, i] = h
+
+        def reading_w1(b, i):
+            h = h_tiles[b, i]
+            cols = slice(i * P, (i + 1) * P)
+            for half in range(halves):
+                js = slice(half * BANK, (half + 1) * BANK)
+                first = psum.tile([P, BANK], F32, name="bank_b")
                 for a in range(k_passes):
                     nc.tensor.matmul_mx(
                         out=first[:],
                         lhsT=w1_codes[a, b][:, cols].bitcast(FP8X4),
                         lhsT_scale=w1_plane[a, b][:, cols],
                         rhs=v_codes[a][:, js].bitcast(FP8X4),
-                        rhs_scale=v_plane[a][:, js],
+                        rhs_scale=v_plane[4 * a : P, js],
                         start=(a == 0), stop=(a == k_passes - 1),
                     )
-                nc.scalar.copy(out=h[:, js], in_=second[:])
                 nc.vector.scalar_tensor_tensor(
                     out=h[:, js], in0=first[:], scalar=b1_sb[:, b, i : i + 1], in1=h[:, js], op0=ALU.add, op1=ALU.min
                 )
-            h_tiles[b, i] = h
+
+        def first_stage(b, i):
+            reading_w2(b, i)
+            reading_w1(b, i)
 
         gate = [kept("gate%d" % b, [P, PACK, PICK], F32) for b in range(r_passes)]
         lit = [kept("lit%d" % b, [P, PACK, PICK], F32) for b in range(r_passes)]
@@ -244,7 +261,7 @@ def tile_list_pack_mismatch_scores_kernel(
             for n in range(n_tiles):
                 cols = slice(n * P, (n + 1) * P)
                 if b == 0:
-                    sums[half, n] = psum.tile([P, 2, HALF], F32, name="acc")
+                    sums[half, n] = psum.tile([P, 2, HALF], F32, name=("bank_a", "bank_b")[half])
                 bank = sums[half, n]
                 nc.tensor.matmul_mx(
                     out=bank[:, 1, :], lhsT=w4_sb[:, b, cols].bitcast(FP8X4), lhsT_scale=w4_plane[:, b, cols],
@@ -263,55 +280,54 @@ def tile_list_pack_mismatch_scores_kernel(
                 nc.vector.tensor_tensor(out=res[:], in0=bank[:, 0, :], in1=res[:], op=ALU.add)
                 nc.sync.dma_start(out=out[n * P : (n + 1) * P, half * HALF : (half + 1) * HALF], in_=res[:])
 
-        gather_plane(0)
         gather_codes(0, 0)
         gather_codes(0, 1)
-        gather_plane(1)
+        deal_w2_plane()
         round_w1(0, 0, 0)
         round_w1(0, 0, 1)
         quantise_w1(0, 0)
         round_w1(1, 0, 0)
-        round_w1(1, 0, 1)
+        round_w1(1, 0, 1, nc.vector.tensor_copy)
         quantise_w1(1, 0)
         gather_codes(1, 0)
         gather_codes(1, 1)
 
         first_stage(0, 0)
         first_stage(0, 1)
-        pick(0, 0)
-        first_stage(0, 2)
         round_w1(0, 1, 0)
         round_w1(0, 1, 1)
         quantise_w1(0, 1)
-        pick(0, 1)
-        first_stage(0, 3)
+        first_stage(0, 2)
         round_w1(1, 1, 0)
         round_w1(1, 1, 1)
         quantise_w1(1, 1)
-        pick(0, 2)
+        pick(0, 0)
+        first_stage(0, 3)
+        pick(0, 1)
         first_stage(1, 0)
-        pick(0, 3)
+        pick(0, 2)
         first_stage(1, 1)
-        pick(1, 0)
+        pick(0, 3)
         first_stage(1, 2)
-        pick(1, 1)
+        pick(1, 0)
         first_stage(1, 3)
         look(0, 0)
         look(0, 1)
         look(0, 2)
         look(0, 3)
-        pick(1, 2)
+        pick(1, 1)
         round_q(0, 0)
         round_w3(0)
         look(1, 0)
         look(1, 1)
-        pick(1, 3, 0, HALF)
+        pick(1, 2)
         quantise_q(0, 0)
         round_q(0, 1)
         look(1, 2)
         look(1, 3, 0, HALF)
         round_w3(1)
         look(1, 3, HALF, PICK)
+        pick(1, 3, 0, HALF)
         quantise_w3(0)
         quantise_q(0, 1)
         second_stage(0, 0)

@@ -2,8 +2,8 @@ from contextlib import ExitStack
 
 import concourse.mybir as mybir
 
-K, T, S, PICK, H, N = 1024, 2048, 1024, 512, 1024, 384
-FLOPS = 2 * 2 * K * H * S + 2 * 2 * H * N * PICK
+K, T, S, M, H, N = 1024, 2048, 1024, 512, 1024, 384
+FLOPS = 2 * (2 * K * H * S) + 2 * (2 * H * N * M)
 
 F32 = mybir.dt.float32
 BF16 = mybir.dt.bfloat16
@@ -19,8 +19,16 @@ ACT = mybir.ActivationFunctionType
 P = 128
 PACK = 4
 PASS = P * PACK
+K_PASSES = K // PASS
+R_PASSES = H // PASS
 BANK = 512
-QUADS = 4
+BANKS = 8
+QUADRANT = 32
+PLANE_ROWS = 4
+PER_COLUMN = 16
+N_TILES = N // P
+PAIR = 2
+HALF = M // 2
 
 
 def tile_list_pack_mismatch_scores_kernel(
@@ -28,317 +36,284 @@ def tile_list_pack_mismatch_scores_kernel(
     slope, shift, light, w3, w4_words, w4_scales, out,
 ):
     nc = tc.nc
-    k_passes = K // PASS
-    r_passes = H // PASS
-    halves = S // BANK
-    n_tiles = N // P
 
     with ExitStack() as ctx:
         lists = ctx.enter_context(tc.tile_pool(name="lists", bufs=1))
         keep = ctx.enter_context(tc.tile_pool(name="keep", bufs=1))
-        ring = ctx.enter_context(tc.tile_pool(name="ring", bufs=3))
-        psum = ctx.enter_context(tc.psum_pool(name="psum", bufs=4))
+        results = ctx.enter_context(tc.tile_pool(name="results", bufs=2 * N_TILES))
+        psum = ctx.enter_context(tc.psum_pool(name="psum", bufs=BANKS))
 
-        def kept(name, shape, dtype):
-            return keep.tile(shape, dtype, name=name, align_bytes=64)
+        def kept(name, shape, dtype, on=None):
+            return keep.tile(shape, dtype, name=name, tag=on or name, align_bytes=64)
 
-        def load_scale_rows(queue, plane, scales):
-            for q in range(QUADS):
-                queue.dma_start(
-                    out=plane[32 * q : 32 * q + 4, :, :].bitcast(I32),
-                    in_=scales[:, 4 * q : 4 * q + 4, :].rearrange("a r c -> r a c").bitcast(I32),
-                )
+        offs_sb = lists.tile([P, S // PER_COLUMN], U16, name="offs_sb")
+        pos1_sb = lists.tile([P, M // PER_COLUMN], U16, name="pos1_sb")
+        pos2_sb = lists.tile([P, M // PER_COLUMN], U16, name="pos2_sb")
 
-        offs_sb = lists.tile([P, S // 16], U16, name="offs_sb")
-        pos1_sb = lists.tile([P, PICK // 16], U16, name="pos1_sb")
-        pos2_sb = lists.tile([P, PICK // 16], U16, name="pos2_sb")
-
-        tab_plane = kept("tab_plane", [P, T], U8)
-        v_plane_moved = kept("v_plane_moved", [P, S], U8)
-        w2_plane_raw = kept("w2_plane_raw", [P, k_passes, H], U8)
-        w4_plane = kept("w4_plane", [P, r_passes, N], U8)
-        for plane in (tab_plane, w2_plane_raw, v_plane_moved, w4_plane):
+        tab_plane = kept("tab_plane", [P, K_PASSES, T], U8)
+        w2_plane_raw = kept("w2_plane_raw", [P, K_PASSES, H], U8)
+        w4_plane = kept("w4_plane", [P, R_PASSES, N], U8)
+        for plane in (tab_plane, w2_plane_raw, w4_plane):
             nc.gpsimd.memset(plane[:].bitcast(I32), 0)
 
-        tab_sb = [kept("tab%d" % a, [P, T], U32) for a in range(k_passes)]
-        w1_raw = {(a, b): kept("w1raw%d%d" % (a, b), [P, PACK, PASS], F32) for a in range(k_passes) for b in range(r_passes)}
-        w2_raw = kept("w2_raw", [P, k_passes, 2 * H], U8)
-        light_sb = [kept("light%d" % b, [P, PACK, PICK], F32) for b in range(r_passes)]
-        w3_raw = [kept("w3raw%d" % b, [P, PACK, N], F32) for b in range(r_passes)]
-        w4_sb = kept("w4_sb", [P, r_passes, N], U32)
-        b1_sb = kept("b1_sb", [P, r_passes, PACK], F32)
-        slope_sb = kept("slope_sb", [P, r_passes, PACK], F32)
-        shift_sb = kept("shift_sb", [P, r_passes, PACK], F32)
+        tab_sb = [kept("tab%d" % a, [P, T], U32) for a in range(K_PASSES)]
+        w1_raw = {
+            (a, g): kept("w1_raw%d%d" % (a, g), [P, PACK, PASS], F32) for a in range(K_PASSES) for g in range(R_PASSES)
+        }
+        w2_raw = kept("w2_raw", [P, K_PASSES, 2 * H], U8)
+        light_sb = [kept("light%d" % g, [P, PACK, M], F32) for g in range(R_PASSES)]
+        w3_raw = [kept("w3_raw%d" % g, [P, PACK, N], F32) for g in range(R_PASSES)]
+        w4_codes = kept("w4_codes", [P, R_PASSES, N], U32)
+        b1_sb = kept("b1_sb", [P, R_PASSES, PACK], F32)
+        slope_sb = kept("slope_sb", [P, R_PASSES, PACK], F32)
+        shift_sb = kept("shift_sb", [P, R_PASSES, PACK], F32)
+
+        def load_plane(plane, scales):
+            for quad in range(P // QUADRANT):
+                nc.sync.dma_start(
+                    out=plane[QUADRANT * quad : QUADRANT * quad + PLANE_ROWS, :, :].bitcast(I32),
+                    in_=scales[:, PLANE_ROWS * quad : PLANE_ROWS * (quad + 1), :].rearrange("a x c -> x a c").bitcast(I32),
+                )
 
         def load_tab(a):
             nc.sync.dma_start(out=tab_sb[a][:].bitcast(I32), in_=tab_words[a].rearrange("p t i -> p (t i)").bitcast(I32))
 
-        def load_w1(a, b):
-            rows = w1[a * PASS : (a + 1) * PASS, b * PASS : (b + 1) * PASS]
-            nc.sync.dma_start(out=w1_raw[a, b][:], in_=rows.rearrange("(p j) c -> p j c", j=PACK))
+        def load_pass(tile, rows):
+            nc.sync.dma_start(out=tile[:], in_=rows.rearrange("(p j) c -> p j c", j=PACK))
 
-        def load_rows(tile, matrix, b):
-            nc.sync.dma_start(out=tile[:], in_=matrix[b * PASS : (b + 1) * PASS, :].rearrange("(p j) c -> p j c", j=PACK))
+        def load_w1(a, g):
+            load_pass(w1_raw[a, g], w1[a * PASS : (a + 1) * PASS, g * PASS : (g + 1) * PASS])
 
-        def load_vector(tile, vec):
-            nc.sync.dma_start(out=tile[:], in_=vec.rearrange("(b p i) -> p b i", b=r_passes, i=PACK))
+        def load_vector(tile, vector):
+            nc.sync.dma_start(out=tile[:], in_=vector.rearrange("(g p t) -> p g t", g=R_PASSES, t=PACK))
 
         nc.sync.dma_start(offs_sb[:], offs)
-        nc.sync.dma_start(out=w2_raw[:].bitcast(I32), in_=w2_words.rearrange("a p c -> p a c").bitcast(I32))
-        load_vector(b1_sb, b1)
-        for q in range(QUADS):
-            nc.sync.dma_start(
-                out=tab_plane[32 * q : 32 * q + 4 * k_passes, :].bitcast(I32),
-                in_=tab_scales[:, 4 * q : 4 * q + 4, :].bitcast(I32),
-            )
         load_tab(0)
+        load_plane(tab_plane, tab_scales)
         load_w1(0, 0)
-        load_scale_rows(nc.sync, w2_plane_raw, w2_scales)
         load_w1(1, 0)
+        load_plane(w2_plane_raw, w2_scales)
+        nc.sync.dma_start(out=w2_raw[:].bitcast(I32), in_=w2_words.rearrange("a p c -> p a c").bitcast(I32))
         load_tab(1)
-        v_plane = kept("v_plane", [P, S], U8)
-        nc.vector.tensor_copy(out=v_plane[:], in_=tab_plane[:].indirect(offs_sb[:]))
-        for q in range(QUADS):
-            nc.sync.dma_start(
-                out=v_plane_moved[32 * q : 32 * q + 4, :].bitcast(I32),
-                in_=v_plane[32 * q + 4 : 32 * q + 8, :].bitcast(I32),
-            )
+        load_vector(b1_sb, b1)
         nc.sync.dma_start(pos2_sb[:], pos2)
-        load_rows(light_sb[0], light, 0)
+        load_pass(light_sb[0], light[:PASS, :])
         nc.sync.dma_start(pos1_sb[:], pos1)
         load_vector(slope_sb, slope)
         load_vector(shift_sb, shift)
         load_w1(0, 1)
         load_w1(1, 1)
-        load_rows(light_sb[1], light, 1)
-        load_rows(w3_raw[0], w3, 0)
-        load_rows(w3_raw[1], w3, 1)
-        nc.sync.dma_start(out=w4_sb[:].bitcast(I32), in_=w4_words.rearrange("a p c i -> p a (c i)").bitcast(I32))
-        load_scale_rows(nc.sync, w4_plane, w4_scales)
+        load_pass(light_sb[1], light[PASS:, :])
+        load_pass(w3_raw[0], w3[:PASS, :])
+        load_pass(w3_raw[1], w3[PASS:, :])
+        nc.sync.dma_start(out=w4_codes[:].bitcast(I32), in_=w4_words.rearrange("g p c i -> p g (c i)").bitcast(I32))
+        load_plane(w4_plane, w4_scales)
 
-        w2_sb = kept("w2_sb", [P, k_passes, 2 * H], U8)
-        w2_plane = kept("w2_plane", [P, k_passes, H], U8)
-        nc.scalar.copy(
-            out=w2_sb[:].bitcast(U16).rearrange("p a (b t m) -> p (a b) t m", b=r_passes, t=PACK),
-            in_=w2_raw[:].bitcast(U16).rearrange("p a (b m t) -> p (a b) t m", b=r_passes, t=PACK),
-        )
-
-        def deal_w2_plane():
-            nc.vector.tensor_copy(
-                out=w2_plane[:].rearrange("p a (b t m) -> p (a b) t m", b=r_passes, t=PACK),
-                in_=w2_plane_raw[:].rearrange("p a (b m t) -> p (a b) t m", b=r_passes, t=PACK),
+        w2_codes = kept("w2_codes", [P, K_PASSES, 2 * H], U8)
+        w2_plane = kept("w2_plane", [P, K_PASSES, H], U8)
+        for g in range(R_PASSES):
+            cols = slice(g * PASS, (g + 1) * PASS)
+            nc.scalar.copy(
+                out=w2_codes[:].bitcast(U16)[:, :, cols].rearrange("p a (t x) -> p a t x", t=PACK),
+                in_=w2_raw[:].bitcast(U16)[:, :, cols].rearrange("p a (x t) -> p a t x", t=PACK),
+            )
+            nc.gpsimd.tensor_copy(
+                out=w2_plane[:, :, cols].rearrange("p a (t x) -> p a t x", t=PACK),
+                in_=w2_plane_raw[:, :, cols].rearrange("p a (x t) -> p a t x", t=PACK),
             )
 
-        v_codes = [kept("vcodes%d" % a, [P, S], U32) for a in range(k_passes)]
+        v_codes = [kept("v_codes%d" % a, [P, S], U32) for a in range(K_PASSES)]
+        v_plane = [kept("v_plane%d" % a, [P, S], U8) for a in range(K_PASSES)]
 
-        def gather_codes(a, half):
-            nc.vector.tensor_copy(
-                out=v_codes[a][:, half * BANK : (half + 1) * BANK],
-                in_=tab_sb[a][:].indirect(offs_sb[:, half * BANK // 16 : (half + 1) * BANK // 16]),
-            )
+        def gather_plane(a):
+            nc.vector.tensor_copy(out=v_plane[a][:], in_=tab_plane[:, a, :].indirect(offs_sb[:]))
 
-        w1_bf = {}
-        w1_codes = {}
-        w1_plane = {}
+        def gather_codes(a):
+            for lo in range(0, S, BANK):
+                entries = offs_sb[:, lo // PER_COLUMN : (lo + BANK) // PER_COLUMN]
+                nc.vector.tensor_copy(out=v_codes[a][:, lo : lo + BANK], in_=tab_sb[a][:].indirect(entries))
 
-        for a in range(k_passes):
-            for b in range(r_passes):
-                w1_bf[a, b] = kept("w1bf%d%d" % (a, b), [P, PASS * PACK], BF16)
-
-        def round_w1(a, b, u, copy=nc.scalar.copy):
-            copy(
-                out=w1_bf[a, b][:].rearrange("p (u e m j) -> p u m j e", u=2, e=2, j=PACK)[:, u],
-                in_=w1_raw[a, b][:].rearrange("p j (m u e) -> p u m j e", u=2, e=2)[:, u],
-            )
-
-        def quantise(name, tile, width):
-            codes = kept(name + "c", [P, width], U32)
-            plane = kept(name + "s", [P, width], U8)
-            nc.vector.quantize_mx(out=codes[:].bitcast(FP8X4), scales=plane[:], in_=tile[:])
+        def quantise(name, rounded, width):
+            codes = kept(name + "_codes", [P, width], U32)
+            plane = kept(name + "_plane", [P, width], U8)
+            nc.vector.quantize_mx(out=codes[:].bitcast(FP8X4), scales=plane[:], in_=rounded[:])
             return codes, plane
 
-        def quantise_w1(a, b):
-            w1_codes[a, b], w1_plane[a, b] = quantise("w1q%d%d" % (a, b), w1_bf[a, b], PASS)
+        w1_rounded = {
+            (a, g): kept("w1_rounded%d%d" % (a, g), [P, PASS * PACK], BF16)
+            for a in range(K_PASSES)
+            for g in range(R_PASSES)
+        }
+        w1_mx = {}
+
+        def prepare_w1(a, g):
+            dealt = w1_rounded[a, g][:].rearrange("p (u e x j) -> p u x j e", u=PACK // PAIR, e=PAIR, j=PACK)
+            raw = w1_raw[a, g][:].rearrange("p j (x u e) -> p u x j e", u=PACK // PAIR, e=PAIR)
+            for u in range(PACK // PAIR):
+                nc.scalar.copy(out=dealt[:, u], in_=raw[:, u])
+            w1_mx[a, g] = quantise("w1_%d%d" % (a, g), w1_rounded[a, g], PASS)
 
         def woven(tile):
-            return tile[:].rearrange("p (c e t) -> p c t e", e=2, t=PACK)
+            return tile[:].rearrange("p (c e t) -> p c t e", e=PAIR, t=PACK)
 
         def by_pairs(tile):
-            return tile[:].rearrange("p t (c e) -> p c t e", e=2)
+            return tile[:].rearrange("p t (c e) -> p c t e", e=PAIR)
 
-        w3_bf = {}
-        w3_q = {}
+        w3_rounded = [kept("w3_rounded%d" % g, [P, N * PACK], BF16) for g in range(R_PASSES)]
+        w3_mx = {}
 
-        def round_w3(b):
-            tile = kept("w3bf%d" % b, [P, N * PACK], BF16)
-            nc.scalar.copy(out=woven(tile), in_=by_pairs(w3_raw[b]))
-            w3_bf[b] = tile
+        def round_w3(g):
+            nc.scalar.copy(out=woven(w3_rounded[g]), in_=by_pairs(w3_raw[g]))
 
-        def quantise_w3(b):
-            w3_q[b] = quantise("w3q%d" % b, w3_bf[b], N)
+        def quantise_w3(g):
+            w3_mx[g] = quantise("w3_%d" % g, w3_rounded[g], N)
 
-        h_tiles = {}
+        h_on = {(0, PACK - K_PASSES + a): "w1_raw%d1" % a for a in range(K_PASSES)}
+        h_sb = {}
 
-        def reading_w2(b, i):
-            h = ring.tile([P, S], F32, name="h", bufs=8)
-            col2 = b * PASS + i * P
-            for half in range(halves):
-                js = slice(half * BANK, (half + 1) * BANK)
-                second = psum.tile([P, BANK], F32, name="bank_a")
-                for a in range(k_passes):
+        def first_stage(g, t):
+            h = kept("h%d%d" % (g, t), [P, S], F32, on=h_on.get((g, t)))
+            place = g * PASS + t * P
+            for lo in range(0, S, BANK):
+                js = slice(lo, lo + BANK)
+                second = psum.tile([P, BANK], F32, name="bank")
+                first = psum.tile([P, BANK], F32, name="bank")
+                for a in range(K_PASSES):
                     nc.tensor.matmul_mx(
                         out=second[:],
-                        lhsT=w2_sb[:, a, 2 * col2 : 2 * (col2 + P)].bitcast(FP4X4),
-                        lhsT_scale=w2_plane[:, a, col2 : col2 + P],
+                        lhsT=w2_codes[:, a, 2 * place : 2 * (place + P)].bitcast(FP4X4),
+                        lhsT_scale=w2_plane[:, a, place : place + P],
                         rhs=v_codes[a][:, js].bitcast(FP8X4),
-                        rhs_scale=(v_plane, v_plane_moved)[a][:, js],
-                        start=(a == 0), stop=(a == k_passes - 1),
+                        rhs_scale=v_plane[a][:, js],
+                        start=(a == 0),
+                        stop=(a == K_PASSES - 1),
                     )
-                nc.scalar.copy(out=h[:, js], in_=second[:])
-            h_tiles[b, i] = h
-
-        def reading_w1(b, i):
-            h = h_tiles[b, i]
-            cols = slice(i * P, (i + 1) * P)
-            for half in range(halves):
-                js = slice(half * BANK, (half + 1) * BANK)
-                first = psum.tile([P, BANK], F32, name="bank_b")
-                for a in range(k_passes):
+                for a in range(K_PASSES):
+                    codes, plane = w1_mx[a, g]
                     nc.tensor.matmul_mx(
                         out=first[:],
-                        lhsT=w1_codes[a, b][:, cols].bitcast(FP8X4),
-                        lhsT_scale=w1_plane[a, b][:, cols],
+                        lhsT=codes[:, t * P : (t + 1) * P].bitcast(FP8X4),
+                        lhsT_scale=plane[:, t * P : (t + 1) * P],
                         rhs=v_codes[a][:, js].bitcast(FP8X4),
-                        rhs_scale=v_plane[4 * a : P, js],
-                        start=(a == 0), stop=(a == k_passes - 1),
+                        rhs_scale=v_plane[a][:, js],
+                        start=(a == 0),
+                        stop=(a == K_PASSES - 1),
                     )
+                nc.scalar.copy(out=h[:, js], in_=second[:])
                 nc.vector.scalar_tensor_tensor(
-                    out=h[:, js], in0=first[:], scalar=b1_sb[:, b, i : i + 1], in1=h[:, js], op0=ALU.add, op1=ALU.min
+                    out=h[:, js], in0=first[:], scalar=b1_sb[:, g, t : t + 1], in1=h[:, js], op0=ALU.add, op1=ALU.min
                 )
+            h_sb[g, t] = h
 
-        def first_stage(b, i):
-            reading_w2(b, i)
-            reading_w1(b, i)
+        gate = [kept("gate0", [P, PACK, M], F32, on="w1_rounded11"), kept("gate1", [P, PACK, M], F32)]
+        lit = [kept("lit%d" % g, [P, PACK, M], F32) for g in range(R_PASSES)]
 
-        gate = [kept("gate%d" % b, [P, PACK, PICK], F32) for b in range(r_passes)]
-        lit = [kept("lit%d" % b, [P, PACK, PICK], F32) for b in range(r_passes)]
-
-        def look(b, i, lo=0, hi=PICK):
+        def look(g, t, lo=0, hi=M):
             nc.scalar.activation(
-                out=gate[b][:, i, lo:hi], in_=h_tiles[b, i][:].indirect(pos1_sb[:, lo // 16 : hi // 16]), func=ACT.Sigmoid,
-                bias=shift_sb[:, b, i : i + 1], scale=slope_sb[:, b, i : i + 1],
+                out=gate[g][:, t, lo:hi],
+                in_=h_sb[g, t][:].indirect(pos1_sb[:, lo // PER_COLUMN : hi // PER_COLUMN]),
+                func=ACT.Sigmoid,
+                bias=shift_sb[:, g, t : t + 1],
+                scale=slope_sb[:, g, t : t + 1],
             )
 
-        def pick(b, i, lo=0, hi=PICK):
+        def pick(g, t, lo=0, hi=M):
             nc.vector.tensor_tensor(
-                out=lit[b][:, i, lo:hi], in0=h_tiles[b, i][:].indirect(pos2_sb[:, lo // 16 : hi // 16]),
-                in1=light_sb[b][:, i, lo:hi], op=ALU.mult,
+                out=lit[g][:, t, lo:hi],
+                in0=h_sb[g, t][:].indirect(pos2_sb[:, lo // PER_COLUMN : hi // PER_COLUMN]),
+                in1=light_sb[g][:, t, lo:hi],
+                op=ALU.mult,
             )
 
-        HALF = PICK // 2
-        q_bf = [kept("qbf%d" % b, [P, PICK * PACK], BF16) for b in range(r_passes)]
-        q_codes = [kept("qc%d" % b, [P, PICK], U32) for b in range(r_passes)]
-        q_plane = [kept("qs%d" % b, [P, PICK], U8) for b in range(r_passes)]
+        q_rounded = [kept("q_rounded%d" % g, [P, M * PACK], BF16) for g in range(R_PASSES)]
+        q_codes = [kept("q_codes%d" % g, [P, M], U32) for g in range(R_PASSES)]
+        q_plane = [kept("q_plane%d" % g, [P, M], U8) for g in range(R_PASSES)]
 
-        def round_q(b, half):
-            pairs = slice(half * HALF // 2, (half + 1) * HALF // 2)
+        def round_q(g, lo, hi):
+            pairs = slice(lo // PAIR, hi // PAIR)
             nc.vector.tensor_tensor(
-                out=woven(q_bf[b])[:, pairs], in0=by_pairs(lit[b])[:, pairs], in1=by_pairs(gate[b])[:, pairs], op=ALU.mult
+                out=woven(q_rounded[g])[:, pairs], in0=by_pairs(lit[g])[:, pairs], in1=by_pairs(gate[g])[:, pairs], op=ALU.mult
             )
 
-        def quantise_q(b, half):
-            ms = slice(half * HALF, (half + 1) * HALF)
+        def quantise_q(g, lo, hi):
             nc.vector.quantize_mx(
-                out=q_codes[b][:, ms].bitcast(FP8X4), scales=q_plane[b][:, ms],
-                in_=q_bf[b][:, half * HALF * PACK : (half + 1) * HALF * PACK],
+                out=q_codes[g][:, lo:hi].bitcast(FP8X4),
+                scales=q_plane[g][:, lo:hi],
+                in_=q_rounded[g][:, lo * PACK : hi * PACK],
             )
 
         sums = {}
 
-        def second_stage(b, half):
-            ms = slice(half * HALF, (half + 1) * HALF)
-            w3_codes, w3_plane = w3_q[b]
-            for n in range(n_tiles):
-                cols = slice(n * P, (n + 1) * P)
-                if b == 0:
-                    sums[half, n] = psum.tile([P, 2, HALF], F32, name=("bank_a", "bank_b")[half])
-                bank = sums[half, n]
-                nc.tensor.matmul_mx(
-                    out=bank[:, 1, :], lhsT=w4_sb[:, b, cols].bitcast(FP8X4), lhsT_scale=w4_plane[:, b, cols],
-                    rhs=q_codes[b][:, ms].bitcast(FP8X4), rhs_scale=q_plane[b][:, ms], start=(b == 0), stop=False,
-                )
-                nc.tensor.matmul_mx(
-                    out=bank[:, 0, :], lhsT=w3_codes[:, cols].bitcast(FP8X4), lhsT_scale=w3_plane[:, cols],
-                    rhs=q_codes[b][:, ms].bitcast(FP8X4), rhs_scale=q_plane[b][:, ms], start=False, stop=(b == r_passes - 1),
-                )
+        def second_stage(g, lo, hi):
+            w3_codes, w3_plane = w3_mx[g]
+            weights = ((w4_codes[:, g, :], w4_plane[:, g, :]), (w3_codes[:], w3_plane[:]))
+            for n in range(N_TILES):
+                if g == 0:
+                    sums[lo, n] = psum.tile([P, 2, hi - lo], F32, name="bank")
+                for which, (codes, plane) in enumerate(weights):
+                    nc.tensor.matmul_mx(
+                        out=sums[lo, n][:, which, :],
+                        lhsT=codes[:, n * P : (n + 1) * P].bitcast(FP8X4),
+                        lhsT_scale=plane[:, n * P : (n + 1) * P],
+                        rhs=q_codes[g][:, lo:hi].bitcast(FP8X4),
+                        rhs_scale=q_plane[g][:, lo:hi],
+                        start=(g == 0 and which == 0),
+                        stop=(g == R_PASSES - 1 and which == 1),
+                    )
 
-        def finish(half):
-            for n in range(n_tiles):
-                bank = sums[half, n]
-                res = ring.tile([P, HALF], F32, name="res", bufs=6)
-                nc.scalar.activation(out=res[:], in_=bank[:, 1, :], func=ACT.Abs)
-                nc.vector.tensor_tensor(out=res[:], in0=bank[:, 0, :], in1=res[:], op=ALU.add)
-                nc.sync.dma_start(out=out[n * P : (n + 1) * P, half * HALF : (half + 1) * HALF], in_=res[:])
+        def finish(lo, hi):
+            for n in range(N_TILES):
+                result = results.tile([P, hi - lo], F32, name="result")
+                nc.scalar.activation(out=result[:], in_=sums[lo, n][:, 0, :], func=ACT.Abs)
+                nc.vector.tensor_tensor(out=result[:], in0=sums[lo, n][:, 1, :], in1=result[:], op=ALU.add)
+                nc.sync.dma_start(out=out[n * P : (n + 1) * P, lo:hi], in_=result[:])
 
-        gather_codes(0, 0)
-        gather_codes(0, 1)
-        deal_w2_plane()
-        round_w1(0, 0, 0)
-        round_w1(0, 0, 1)
-        quantise_w1(0, 0)
-        round_w1(1, 0, 0)
-        round_w1(1, 0, 1, nc.vector.tensor_copy)
-        quantise_w1(1, 0)
-        gather_codes(1, 0)
-        gather_codes(1, 1)
+        warm = kept("warm", [P, 2], F32)
+        nc.vector.memset(warm[:, 0:1], 0.0)
+        nc.scalar.activation(out=warm[:, 1:2], in_=warm[:, 0:1], func=ACT.Sigmoid)
 
-        first_stage(0, 0)
-        first_stage(0, 1)
-        round_w1(0, 1, 0)
-        round_w1(0, 1, 1)
-        quantise_w1(0, 1)
-        first_stage(0, 2)
-        round_w1(1, 1, 0)
-        round_w1(1, 1, 1)
-        quantise_w1(1, 1)
-        pick(0, 0)
-        first_stage(0, 3)
-        pick(0, 1)
-        first_stage(1, 0)
-        pick(0, 2)
-        first_stage(1, 1)
-        pick(0, 3)
-        first_stage(1, 2)
-        pick(1, 0)
-        first_stage(1, 3)
-        look(0, 0)
-        look(0, 1)
-        look(0, 2)
-        look(0, 3)
-        pick(1, 1)
-        round_q(0, 0)
-        round_w3(0)
+        gather_codes(0)
+        gather_plane(0)
+        gather_plane(1)
+        prepare_w1(0, 0)
+        prepare_w1(1, 0)
+        gather_codes(1)
+
+        slices = [(g, t) for g in range(R_PASSES) for t in range(PACK)]
+        for s, (g, t) in enumerate(slices):
+            first_stage(g, t)
+            if 1 <= s <= K_PASSES:
+                prepare_w1(s - 1, 1)
+            if s >= len(slices) - 2:
+                look(0, 2 * (s % 2))
+                look(0, 2 * (s % 2) + 1)
+            if s >= 1:
+                pick(*slices[s - 1])
+
+        left, right = (0, HALF), (HALF, M)
+        last = slices[-1]
         look(1, 0)
         look(1, 1)
-        pick(1, 2)
-        quantise_q(0, 0)
-        round_q(0, 1)
+        round_w3(0)
         look(1, 2)
-        look(1, 3, 0, HALF)
+        look(*last, *left)
+        look(*last, *right)
         round_w3(1)
-        look(1, 3, HALF, PICK)
-        pick(1, 3, 0, HALF)
+
+        round_q(0, *left)
+        round_q(0, *right)
+        pick(*last, *left)
         quantise_w3(0)
-        quantise_q(0, 1)
-        second_stage(0, 0)
-        second_stage(0, 1)
-        round_q(1, 0)
-        pick(1, 3, HALF, PICK)
-        quantise_q(1, 0)
+        quantise_q(0, 0, M)
+        second_stage(0, *left)
+        second_stage(0, *right)
+        round_q(1, *left)
+        pick(*last, *right)
+        quantise_q(1, *left)
+        round_q(1, *right)
         quantise_w3(1)
-        second_stage(1, 0)
-        round_q(1, 1)
-        quantise_q(1, 1)
-        second_stage(1, 1)
-        finish(0)
-        finish(1)
+        second_stage(1, *left)
+        quantise_q(1, *right)
+        second_stage(1, *right)
+        finish(*left)
+        finish(*right)

@@ -28,6 +28,7 @@ PLANE_ROWS = 4
 PER_COLUMN = 16
 N_TILES = N // P
 PAIR = 2
+RUN = 4
 HALF = M // 2
 
 
@@ -110,7 +111,10 @@ def tile_list_pack_mismatch_scores_kernel(
         load_plane(w4_plane, w4_scales)
 
         w2_codes = kept("w2_codes", [P, K_PASSES, 2 * H], U8)
-        w2_plane = kept("w2_plane", [P, K_PASSES, H], U8)
+        w2_plane = [
+            kept("w2_plane0", [P, K_PASSES, PASS], U8),
+            kept("w2_plane1", [P, K_PASSES, PASS], U8, on="tab%d" % (K_PASSES - 1)),
+        ]
         for g in range(R_PASSES):
             cols = slice(g * PASS, (g + 1) * PASS)
             nc.scalar.copy(
@@ -118,7 +122,7 @@ def tile_list_pack_mismatch_scores_kernel(
                 in_=w2_raw[:].bitcast(U16)[:, :, cols].rearrange("p a (x t) -> p a t x", t=PACK),
             )
             nc.gpsimd.tensor_copy(
-                out=w2_plane[:, :, cols].rearrange("p a (t x) -> p a t x", t=PACK),
+                out=w2_plane[g][:].rearrange("p a (t x) -> p a t x", t=PACK),
                 in_=w2_plane_raw[:, :, cols].rearrange("p a (x t) -> p a t x", t=PACK),
             )
 
@@ -154,16 +158,16 @@ def tile_list_pack_mismatch_scores_kernel(
             w1_mx[a, g] = quantise("w1_%d%d" % (a, g), w1_rounded[a, g], PASS)
 
         def woven(tile):
-            return tile[:].rearrange("p (c e t) -> p c t e", e=PAIR, t=PACK)
+            return tile[:].rearrange("p (c e t) -> p c t e", e=RUN, t=PACK)
 
-        def by_pairs(tile):
-            return tile[:].rearrange("p t (c e) -> p c t e", e=PAIR)
+        def by_runs(tile):
+            return tile[:].rearrange("p t (c e) -> p c t e", e=RUN)
 
         w3_rounded = [kept("w3_rounded%d" % g, [P, N * PACK], BF16) for g in range(R_PASSES)]
         w3_mx = {}
 
         def round_w3(g):
-            nc.scalar.copy(out=woven(w3_rounded[g]), in_=by_pairs(w3_raw[g]))
+            nc.scalar.copy(out=woven(w3_rounded[g]), in_=by_runs(w3_raw[g]))
 
         def quantise_w3(g):
             w3_mx[g] = quantise("w3_%d" % g, w3_rounded[g], N)
@@ -182,7 +186,7 @@ def tile_list_pack_mismatch_scores_kernel(
                     nc.tensor.matmul_mx(
                         out=second[:],
                         lhsT=w2_codes[:, a, 2 * place : 2 * (place + P)].bitcast(FP4X4),
-                        lhsT_scale=w2_plane[:, a, place : place + P],
+                        lhsT_scale=w2_plane[g][:, a, t * P : (t + 1) * P],
                         rhs=v_codes[a][:, js].bitcast(FP8X4),
                         rhs_scale=v_plane[a][:, js],
                         start=(a == 0),
@@ -230,9 +234,9 @@ def tile_list_pack_mismatch_scores_kernel(
         q_plane = [kept("q_plane%d" % g, [P, M], U8) for g in range(R_PASSES)]
 
         def round_q(g, lo, hi):
-            pairs = slice(lo // PAIR, hi // PAIR)
+            runs = slice(lo // RUN, hi // RUN)
             nc.vector.tensor_tensor(
-                out=woven(q_rounded[g])[:, pairs], in0=by_pairs(lit[g])[:, pairs], in1=by_pairs(gate[g])[:, pairs], op=ALU.mult
+                out=woven(q_rounded[g])[:, runs], in0=by_runs(lit[g])[:, runs], in1=by_runs(gate[g])[:, runs], op=ALU.mult
             )
 
         def quantise_q(g, lo, hi):

from contextlib import ExitStack

import concourse.mybir as mybir

K, T, S, M, H, N = 1024, 2048, 1024, 512, 1024, 384
FLOPS = 2 * (2 * K * H * S) + 2 * (2 * H * N * M)

F32 = mybir.dt.float32
BF16 = mybir.dt.bfloat16
I32 = mybir.dt.int32
U32 = mybir.dt.uint32
U16 = mybir.dt.uint16
U8 = mybir.dt.uint8
FP8X4 = mybir.dt.float8_e4m3fn_x4
FP4X4 = mybir.dt.float4_e2m1fn_x4
ALU = mybir.AluOpType
ACT = mybir.ActivationFunctionType

P = 128
PACK = 4
PASS = P * PACK
K_PASSES = K // PASS
R_PASSES = H // PASS
BANK = 512
BANKS = 8
QUADRANT = 32
PLANE_ROWS = 4
PER_COLUMN = 16
N_TILES = N // P
PAIR = 2
RUN = 4
HALF = M // 2


def tile_list_pack_mismatch_scores_kernel(
    tc, tab_words, tab_scales, offs, pos1, pos2, w1, b1, w2_words, w2_scales,
    slope, shift, light, w3, w4_words, w4_scales, out,
):
    nc = tc.nc

    with ExitStack() as ctx:
        lists = ctx.enter_context(tc.tile_pool(name="lists", bufs=1))
        keep = ctx.enter_context(tc.tile_pool(name="keep", bufs=1))
        results = ctx.enter_context(tc.tile_pool(name="results", bufs=2 * N_TILES))
        psum = ctx.enter_context(tc.psum_pool(name="psum", bufs=BANKS))

        def kept(name, shape, dtype, on=None):
            return keep.tile(shape, dtype, name=name, tag=on or name, align_bytes=64)

        offs_sb = lists.tile([P, S // PER_COLUMN], U16, name="offs_sb")
        pos1_sb = lists.tile([P, M // PER_COLUMN], U16, name="pos1_sb")
        pos2_sb = lists.tile([P, M // PER_COLUMN], U16, name="pos2_sb")

        tab_plane = kept("tab_plane", [P, K_PASSES, T], U8)
        w2_plane_raw = kept("w2_plane_raw", [P, K_PASSES, H], U8)
        w4_plane = kept("w4_plane", [P, R_PASSES, N], U8)
        for plane in (tab_plane, w2_plane_raw, w4_plane):
            nc.gpsimd.memset(plane[:].bitcast(I32), 0)

        tab_sb = [kept("tab%d" % a, [P, T], U32) for a in range(K_PASSES)]
        w1_raw = {
            (a, g): kept("w1_raw%d%d" % (a, g), [P, PACK, PASS], F32) for a in range(K_PASSES) for g in range(R_PASSES)
        }
        w2_raw = kept("w2_raw", [P, K_PASSES, 2 * H], U8)
        light_sb = [kept("light%d" % g, [P, PACK, M], F32) for g in range(R_PASSES)]
        w3_raw = [kept("w3_raw%d" % g, [P, PACK, N], F32) for g in range(R_PASSES)]
        w4_codes = kept("w4_codes", [P, R_PASSES, N], U32)
        b1_sb = kept("b1_sb", [P, R_PASSES, PACK], F32)
        slope_sb = kept("slope_sb", [P, R_PASSES, PACK], F32)
        shift_sb = kept("shift_sb", [P, R_PASSES, PACK], F32)

        def load_plane(plane, scales):
            for quad in range(P // QUADRANT):
                nc.sync.dma_start(
                    out=plane[QUADRANT * quad : QUADRANT * quad + PLANE_ROWS, :, :].bitcast(I32),
                    in_=scales[:, PLANE_ROWS * quad : PLANE_ROWS * (quad + 1), :].rearrange("a x c -> x a c").bitcast(I32),
                )

        def load_tab(a):
            nc.sync.dma_start(out=tab_sb[a][:].bitcast(I32), in_=tab_words[a].rearrange("p t i -> p (t i)").bitcast(I32))

        def load_pass(tile, rows):
            nc.sync.dma_start(out=tile[:], in_=rows.rearrange("(p j) c -> p j c", j=PACK))

        def load_w1(a, g):
            load_pass(w1_raw[a, g], w1[a * PASS : (a + 1) * PASS, g * PASS : (g + 1) * PASS])

        def load_vector(tile, vector):
            nc.sync.dma_start(out=tile[:], in_=vector.rearrange("(g p t) -> p g t", g=R_PASSES, t=PACK))

        nc.sync.dma_start(offs_sb[:], offs)
        load_tab(0)
        load_plane(tab_plane, tab_scales)
        load_w1(0, 0)
        load_w1(1, 0)
        load_plane(w2_plane_raw, w2_scales)
        nc.sync.dma_start(out=w2_raw[:].bitcast(I32), in_=w2_words.rearrange("a p c -> p a c").bitcast(I32))
        load_tab(1)
        load_vector(b1_sb, b1)
        nc.sync.dma_start(pos2_sb[:], pos2)
        load_pass(light_sb[0], light[:PASS, :])
        nc.sync.dma_start(pos1_sb[:], pos1)
        load_vector(slope_sb, slope)
        load_vector(shift_sb, shift)
        load_w1(0, 1)
        load_w1(1, 1)
        load_pass(light_sb[1], light[PASS:, :])
        load_pass(w3_raw[0], w3[:PASS, :])
        load_pass(w3_raw[1], w3[PASS:, :])
        nc.sync.dma_start(out=w4_codes[:].bitcast(I32), in_=w4_words.rearrange("g p c i -> p g (c i)").bitcast(I32))
        load_plane(w4_plane, w4_scales)

        w2_codes = kept("w2_codes", [P, K_PASSES, 2 * H], U8)
        w2_plane = [
            kept("w2_plane0", [P, K_PASSES, PASS], U8),
            kept("w2_plane1", [P, K_PASSES, PASS], U8, on="tab%d" % (K_PASSES - 1)),
        ]
        for g in range(R_PASSES):
            cols = slice(g * PASS, (g + 1) * PASS)
            nc.scalar.copy(
                out=w2_codes[:].bitcast(U16)[:, :, cols].rearrange("p a (t x) -> p a t x", t=PACK),
                in_=w2_raw[:].bitcast(U16)[:, :, cols].rearrange("p a (x t) -> p a t x", t=PACK),
            )
            nc.gpsimd.tensor_copy(
                out=w2_plane[g][:].rearrange("p a (t x) -> p a t x", t=PACK),
                in_=w2_plane_raw[:, :, cols].rearrange("p a (x t) -> p a t x", t=PACK),
            )

        v_codes = [kept("v_codes%d" % a, [P, S], U32) for a in range(K_PASSES)]
        v_plane = [kept("v_plane%d" % a, [P, S], U8) for a in range(K_PASSES)]

        def gather_plane(a):
            nc.vector.tensor_copy(out=v_plane[a][:], in_=tab_plane[:, a, :].indirect(offs_sb[:]))

        def gather_codes(a):
            for lo in range(0, S, BANK):
                entries = offs_sb[:, lo // PER_COLUMN : (lo + BANK) // PER_COLUMN]
                nc.vector.tensor_copy(out=v_codes[a][:, lo : lo + BANK], in_=tab_sb[a][:].indirect(entries))

        def quantise(name, rounded, width):
            codes = kept(name + "_codes", [P, width], U32)
            plane = kept(name + "_plane", [P, width], U8)
            nc.vector.quantize_mx(out=codes[:].bitcast(FP8X4), scales=plane[:], in_=rounded[:])
            return codes, plane

        w1_rounded = {
            (a, g): kept("w1_rounded%d%d" % (a, g), [P, PASS * PACK], BF16)
            for a in range(K_PASSES)
            for g in range(R_PASSES)
        }
        w1_mx = {}

        def prepare_w1(a, g):
            dealt = w1_rounded[a, g][:].rearrange("p (u e x j) -> p u x j e", u=PACK // PAIR, e=PAIR, j=PACK)
            raw = w1_raw[a, g][:].rearrange("p j (x u e) -> p u x j e", u=PACK // PAIR, e=PAIR)
            for u in range(PACK // PAIR):
                nc.scalar.copy(out=dealt[:, u], in_=raw[:, u])
            w1_mx[a, g] = quantise("w1_%d%d" % (a, g), w1_rounded[a, g], PASS)

        def woven(tile):
            return tile[:].rearrange("p (c e t) -> p c t e", e=RUN, t=PACK)

        def by_runs(tile):
            return tile[:].rearrange("p t (c e) -> p c t e", e=RUN)

        w3_rounded = [kept("w3_rounded%d" % g, [P, N * PACK], BF16) for g in range(R_PASSES)]
        w3_mx = {}

        def round_w3(g):
            nc.scalar.copy(out=woven(w3_rounded[g]), in_=by_runs(w3_raw[g]))

        def quantise_w3(g):
            w3_mx[g] = quantise("w3_%d" % g, w3_rounded[g], N)

        h_on = {(0, PACK - K_PASSES + a): "w1_raw%d1" % a for a in range(K_PASSES)}
        h_sb = {}

        def first_stage(g, t):
            h = kept("h%d%d" % (g, t), [P, S], F32, on=h_on.get((g, t)))
            place = g * PASS + t * P
            for lo in range(0, S, BANK):
                js = slice(lo, lo + BANK)
                second = psum.tile([P, BANK], F32, name="bank")
                first = psum.tile([P, BANK], F32, name="bank")
                for a in range(K_PASSES):
                    nc.tensor.matmul_mx(
                        out=second[:],
                        lhsT=w2_codes[:, a, 2 * place : 2 * (place + P)].bitcast(FP4X4),
                        lhsT_scale=w2_plane[g][:, a, t * P : (t + 1) * P],
                        rhs=v_codes[a][:, js].bitcast(FP8X4),
                        rhs_scale=v_plane[a][:, js],
                        start=(a == 0),
                        stop=(a == K_PASSES - 1),
                    )
                for a in range(K_PASSES):
                    codes, plane = w1_mx[a, g]
                    nc.tensor.matmul_mx(
                        out=first[:],
                        lhsT=codes[:, t * P : (t + 1) * P].bitcast(FP8X4),
                        lhsT_scale=plane[:, t * P : (t + 1) * P],
                        rhs=v_codes[a][:, js].bitcast(FP8X4),
                        rhs_scale=v_plane[a][:, js],
                        start=(a == 0),
                        stop=(a == K_PASSES - 1),
                    )
                nc.scalar.copy(out=h[:, js], in_=second[:])
                nc.vector.scalar_tensor_tensor(
                    out=h[:, js], in0=first[:], scalar=b1_sb[:, g, t : t + 1], in1=h[:, js], op0=ALU.add, op1=ALU.min
                )
            h_sb[g, t] = h

        gate = [kept("gate0", [P, PACK, M], F32, on="w1_rounded11"), kept("gate1", [P, PACK, M], F32)]
        lit = [kept("lit%d" % g, [P, PACK, M], F32) for g in range(R_PASSES)]

        def look(g, t, lo=0, hi=M):
            nc.scalar.activation(
                out=gate[g][:, t, lo:hi],
                in_=h_sb[g, t][:].indirect(pos1_sb[:, lo // PER_COLUMN : hi // PER_COLUMN]),
                func=ACT.Sigmoid,
                bias=shift_sb[:, g, t : t + 1],
                scale=slope_sb[:, g, t : t + 1],
            )

        def pick(g, t, lo=0, hi=M):
            nc.vector.tensor_tensor(
                out=lit[g][:, t, lo:hi],
                in0=h_sb[g, t][:].indirect(pos2_sb[:, lo // PER_COLUMN : hi // PER_COLUMN]),
                in1=light_sb[g][:, t, lo:hi],
                op=ALU.mult,
            )

        q_rounded = [kept("q_rounded%d" % g, [P, M * PACK], BF16) for g in range(R_PASSES)]
        q_codes = [kept("q_codes%d" % g, [P, M], U32) for g in range(R_PASSES)]
        q_plane = [kept("q_plane%d" % g, [P, M], U8) for g in range(R_PASSES)]

        def round_q(g, lo, hi):
            runs = slice(lo // RUN, hi // RUN)
            nc.vector.tensor_tensor(
                out=woven(q_rounded[g])[:, runs], in0=by_runs(lit[g])[:, runs], in1=by_runs(gate[g])[:, runs], op=ALU.mult
            )

        def quantise_q(g, lo, hi):
            nc.vector.quantize_mx(
                out=q_codes[g][:, lo:hi].bitcast(FP8X4),
                scales=q_plane[g][:, lo:hi],
                in_=q_rounded[g][:, lo * PACK : hi * PACK],
            )

        sums = {}

        def second_stage(g, lo, hi):
            w3_codes, w3_plane = w3_mx[g]
            weights = ((w4_codes[:, g, :], w4_plane[:, g, :]), (w3_codes[:], w3_plane[:]))
            for n in range(N_TILES):
                if g == 0:
                    sums[lo, n] = psum.tile([P, 2, hi - lo], F32, name="bank")
                for which, (codes, plane) in enumerate(weights):
                    nc.tensor.matmul_mx(
                        out=sums[lo, n][:, which, :],
                        lhsT=codes[:, n * P : (n + 1) * P].bitcast(FP8X4),
                        lhsT_scale=plane[:, n * P : (n + 1) * P],
                        rhs=q_codes[g][:, lo:hi].bitcast(FP8X4),
                        rhs_scale=q_plane[g][:, lo:hi],
                        start=(g == 0 and which == 0),
                        stop=(g == R_PASSES - 1 and which == 1),
                    )

        def finish(lo, hi):
            for n in range(N_TILES):
                result = results.tile([P, hi - lo], F32, name="result")
                nc.scalar.activation(out=result[:], in_=sums[lo, n][:, 0, :], func=ACT.Abs)
                nc.vector.tensor_tensor(out=result[:], in0=sums[lo, n][:, 1, :], in1=result[:], op=ALU.add)
                nc.sync.dma_start(out=out[n * P : (n + 1) * P, lo:hi], in_=result[:])

        warm = kept("warm", [P, 2], F32)
        nc.vector.memset(warm[:, 0:1], 0.0)
        nc.scalar.activation(out=warm[:, 1:2], in_=warm[:, 0:1], func=ACT.Sigmoid)

        gather_codes(0)
        gather_plane(0)
        gather_plane(1)
        prepare_w1(0, 0)
        prepare_w1(1, 0)
        gather_codes(1)

        slices = [(g, t) for g in range(R_PASSES) for t in range(PACK)]
        for s, (g, t) in enumerate(slices):
            first_stage(g, t)
            if 1 <= s <= K_PASSES:
                prepare_w1(s - 1, 1)
            if s >= len(slices) - 2:
                look(0, 2 * (s % 2))
                look(0, 2 * (s % 2) + 1)
            if s >= 1:
                pick(*slices[s - 1])

        left, right = (0, HALF), (HALF, M)
        last = slices[-1]
        look(1, 0)
        look(1, 1)
        round_w3(0)
        look(1, 2)
        look(*last, *left)
        look(*last, *right)
        round_w3(1)

        round_q(0, *left)
        round_q(0, *right)
        pick(*last, *left)
        quantise_w3(0)
        quantise_q(0, 0, M)
        second_stage(0, *left)
        second_stage(0, *right)
        round_q(1, *left)
        pick(*last, *right)
        quantise_q(1, *left)
        round_q(1, *right)
        quantise_w3(1)
        second_stage(1, *left)
        quantise_q(1, *right)
        second_stage(1, *right)
        finish(*left)
        finish(*right)
